import numpy as np
import ml_dtypes


def mxq(x, axis, fmt="e4m3"):
    dtype, down = {"e4m3": (ml_dtypes.float8_e4m3fn, 7), "e5m2": (ml_dtypes.float8_e5m2, 14)}[fmt]
    v = np.moveaxis(np.asarray(x, np.float32).astype(ml_dtypes.bfloat16).astype(np.float64), axis, -1)
    blocks = v.reshape(v.shape[:-1] + (-1, 32))
    amax = np.abs(blocks).max(-1, keepdims=True)
    byte = np.maximum(np.where(amax > 0, np.frexp(amax)[1] - 1 + 127, 0) - down, 1)
    scale = np.exp2(byte - 127.0)
    codes = (blocks / scale).astype(np.float32).astype(dtype).astype(np.float64)
    return np.moveaxis((codes * scale).reshape(v.shape), -1, axis)


WIDE = False


def mx_kscale(k):
    if not WIDE:
        return np.ones(k)
    levels = np.array([10, -10, 5, -5, 0])
    if k % 512:
        return np.exp2(np.random.permutation(np.resize(levels, k // 32))).repeat(32)
    a = np.empty((k // 512, 16))
    for p in range(k // 512):
        a[p, :8] = np.random.permutation(np.resize(levels, 8))
        for g in range(8):
            far = levels[np.abs(levels - a[p, g]) >= 10]
            a[p, g + 8] = far[np.random.randint(len(far))]
    return np.exp2(a.ravel()).repeat(32)


BF16 = ml_dtypes.bfloat16


def bf(x):
    return np.asarray(x, np.float32).astype(BF16)


def f64(x):
    return np.asarray(x).astype(np.float64)


E2M1 = np.array([0.0, 0.5, 1.0, 1.5, 2.0, 3.0, 4.0, 6.0, -0.0, -0.5, -1.0, -1.5, -2.0, -3.0, -4.0, -6.0])


def pack_weight(w, fmt):
    k, n = w.shape
    w = f64(bf(w)).reshape(k // 32, 32, n)
    amax = np.abs(w).max(1)
    if fmt == "e4m3":
        byte = np.frexp(amax)[1] - 1 + 127 - 7
    else:
        mant, ex = np.frexp(amax / 6.0)
        byte = np.where(mant > 0.5, ex, ex - 1) + 127
    byte = np.clip(np.where(amax > 0, byte, 1), 1, 254)
    scaled = (w * np.exp2(127.0 - byte)[:, None, :]).reshape(k, n).astype(np.float32)
    by_word = np.ascontiguousarray(scaled.reshape(k // 512, 128, 4, n).transpose(0, 1, 3, 2))
    if fmt == "e4m3":
        words = by_word.astype(ml_dtypes.float8_e4m3fn).view(np.uint8)
    else:
        c = by_word.astype(ml_dtypes.float4_e2m1fn).view(np.uint8) & 0xF
        words = c[..., 0::2] | (c[..., 1::2] << 4)
    return np.ascontiguousarray(words), np.ascontiguousarray(byte.astype(np.uint8).reshape(k // 512, 16, n))


def unpack_weight(words, scales, fmt):
    g, p, n, _ = words.shape
    if fmt == "e4m3":
        vals = np.ascontiguousarray(words).view(ml_dtypes.float8_e4m3fn).astype(np.float64)
    else:
        nib = np.empty((g, p, n, 4), np.uint8)
        nib[..., 0::2] = words & 0xF
        nib[..., 1::2] = words >> 4
        vals = E2M1[nib]
    vals = vals * np.repeat(np.exp2(scales.astype(np.float64) - 127.0), 8, axis=1)[..., None]
    return vals.transpose(0, 1, 3, 2).reshape(g * 512, n)
def pack4(w):
    words, scales = pack_weight(w, "e2m1")
    return words.reshape(words.shape[0], 128, -1), scales


def unpack4(words, scales):
    return unpack_weight(words.reshape(words.shape[0], 128, -1, 2), scales, "e2m1")


M, K, F, N = 1024, 1024, 2048, 1024


def setup_inputs():
    s, t = mx_kscale(K), mx_kscale(F)
    energy = np.exp(np.random.standard_normal(K))
    loudness = np.exp(0.5 * np.random.standard_normal(M))
    act = np.maximum(np.random.standard_normal((K, M)), 0.0)
    a_words, a_scales = pack4(act ** 2 * energy[:, None] * loudness * s[:, None])
    step_sq = np.exp(np.random.standard_normal((K, F))) / K
    d_words, d_scales = pack4(step_sq / s[:, None] * t)
    sens_sq = 0.3 * np.exp(1.5 * np.random.standard_normal((F, N))) / F
    j_words, j_scales = pack_weight(sens_sq / t[:, None], "e4m3")
    return {"a_words": a_words, "a_scales": a_scales,
            "d_words": d_words, "d_scales": d_scales,
            "noise_floor": bf(0.5 * np.random.standard_normal(F) ** 2 * t),
            "slope_sq": bf(np.random.standard_normal((M, F)) ** 2),
            "j_words": j_words, "j_scales": j_scales}


def reference(a_words, a_scales, d_words, d_scales, noise_floor, slope_sq, j_words, j_scales):
    a = unpack4(a_words, a_scales)
    d = unpack4(d_words, d_scales)
    j = unpack_weight(j_words, j_scales, "e4m3")
    h = a.T @ d
    v = (h + f64(noise_floor)) * f64(slope_sq)
    return mxq(v, 1, "e4m3") @ j

@@ -1,0 +1,237 @@
+from contextlib import ExitStack
+
+import concourse.mybir as mybir
+from concourse.masks import make_identity
+
+M, K, F, N = 1024, 1024, 2048, 1024
+FLOPS = 2 * M * K * F + 2 * M * F * N
+
+F32 = mybir.dt.float32
+BF16 = mybir.dt.bfloat16
+I32 = mybir.dt.int32
+U32 = mybir.dt.uint32
+U8 = mybir.dt.uint8
+FP4X4 = mybir.dt.float4_e2m1fn_x4
+FP8X4 = mybir.dt.float8_e4m3fn_x4
+ADD = mybir.AluOpType.add
+MULT = mybir.AluOpType.mult
+
+P = 128
+KG = K // 512
+FG = F // 512
+MT = M // P
+NH = N // 512
+
+
+def tile_rounding_variance_propagation_s4_kernel(
+    tc, a_words, a_scales, d_words, d_scales, noise_floor, slope_sq, j_words, j_scales, out
+):
+    nc = tc.nc
+    with ExitStack() as ctx:
+        keep = ctx.enter_context(tc.tile_pool(name="keep", bufs=1))
+        work = ctx.enter_context(tc.tile_pool(name="work", bufs=2))
+        ypool = ctx.enter_context(tc.tile_pool(name="ypool", bufs=4))
+        psum = ctx.enter_context(tc.psum_pool(name="psum", bufs=2))
+        ctx.enter_context(tc.manual_schedule())
+
+        a_lo = keep.tile([P, KG, 1024], U8, align_bytes=64)
+        a_hi = keep.tile([P, KG, 1024], U8, align_bytes=64)
+        d_lo = keep.tile([P, KG, 2048], U8, align_bytes=64)
+        d_hi = keep.tile([P, KG, 2048], U8, align_bytes=64)
+        a_sc = keep.tile([P, KG, M], U8, align_bytes=64)
+        d_sc = keep.tile([P, KG, F], U8, align_bytes=64)
+        j_sb = keep.tile([P, FG, 4 * N], U8, align_bytes=64)
+        j_sc = keep.tile([P, N], U8, align_bytes=64)
+        nf_col = keep.tile([P, 16], BF16, align_bytes=64)
+        nf_row = keep.tile([P, F], BF16, align_bytes=64)
+        ident_h = keep.tile([P, P], BF16, align_bytes=64)
+        ident_f = keep.tile([P, P], F32, align_bytes=64)
+        slopes = [keep.tile([P, F], BF16, align_bytes=64, name="slope%d" % mt) for mt in range(MT)]
+        warm = keep.tile([P, 8], F32, align_bytes=64)
+
+        nc.vector.memset(warm[:], 0.0)
+        nc.vector.memset(d_sc[:].rearrange("p g n -> p (g n)").bitcast(I32), 0)
+        nc.vector.memset(a_sc[:].rearrange("p g n -> p (g n)").bitcast(I32), 0)
+        nc.vector.memset(j_sc[:].bitcast(I32), 0)
+
+        aw = a_words.bitcast(I32).rearrange("g p n -> p g n")
+        dw = d_words.bitcast(I32).rearrange("g p n -> p g n")
+        asw = a_scales.bitcast(I32).rearrange("g r n -> r g n")
+        dsw = d_scales.bitcast(I32).rearrange("g r n -> r g n")
+        jsw = j_scales.bitcast(I32)
+        nc.sync.dma_start(out=nf_col[:], in_=noise_floor.rearrange("(p c) -> p c", c=16))
+        nc.sync.dma_start(out=a_lo[:].bitcast(I32), in_=aw[:, :, 0:256])
+        nc.sync.dma_start(out=d_lo[:].bitcast(I32), in_=dw[:, :, 0:512])
+        nc.sync.dma_start(out=d_hi[:].bitcast(I32), in_=dw[:, :, 512:1024])
+        make_identity(nc, ident_h[:])
+        for q in range(4):
+            nc.scalar.dma_start(
+                out=d_sc[32 * q : 32 * q + 4, :, :].bitcast(I32), in_=dsw[4 * q : 4 * q + 4, :, :]
+            )
+        for q in range(4):
+            nc.gpsimd.dma_start(
+                out=a_sc[32 * q : 32 * q + 4, :, :].bitcast(I32), in_=asw[4 * q : 4 * q + 4, :, :]
+            )
+        make_identity(nc, ident_f[:])
+        for q in range(4):
+            nc.gpsimd.dma_start(
+                out=j_sc[32 * q : 32 * q + 16, :].bitcast(I32), in_=jsw[:, 4 * q : 4 * q + 4, :]
+            )
+        nc.scalar.copy(out=warm[:, 4:5], in_=warm[:, 0:1])
+
+        def load_slope(mt):
+            nc.sync.dma_start(out=slopes[mt][:], in_=slope_sq[mt * P : (mt + 1) * P, :])
+
+        load_slope(0)
+        load_slope(1)
+        nc.sync.dma_start(out=a_hi[:].bitcast(I32), in_=aw[:, :, 256:512])
+        for g in range(FG):
+            nc.sync.dma_start(
+                out=j_sb[:, g, :].bitcast(I32),
+                in_=j_words[g].rearrange("p n t -> p (n t)").bitcast(I32),
+            )
+        for mt in range(2, MT):
+            load_slope(mt)
+
+        for h in range(2):
+            nf_ps = psum.tile([P, 8, P], BF16, tag="vt", name="nf_ps")
+            for c in range(8):
+                col = 8 * h + c
+                nc.tensor.transpose(
+                    nf_ps[:, c, :], nf_col[:, col : col + 1].to_broadcast([P, P]), ident_h[:]
+                )
+            dst = nf_row[:].rearrange("q (p c) -> q p c", c=16)[:, :, 8 * h : 8 * h + 8]
+            src = nf_ps[:].rearrange("q c p -> q p c")
+            if h == 0:
+                nc.vector.tensor_copy(out=dst, in_=src)
+            else:
+                nc.scalar.copy(out=dst, in_=src)
+
+        hs = {}
+        tmps = {}
+        vs = {}
+        vts = {}
+        vqs = {}
+        codes = {}
+
+        def upe(ap):
+            return ap.rearrange("q (p u e) -> q u p e", u=2, e=2)
+
+        def packed(ap):
+            return ap.rearrange("q (u p e) -> q u p e", u=2, e=2)
+
+        def s1(mt):
+            a_sb = a_lo if mt < 4 else a_hi
+            m0 = (mt % 4) * P
+            for g in range(FG):
+                h_ps = psum.tile([P, 512], F32, tag="h", bufs=4, name="h_ps")
+                hs[mt, g] = h_ps
+                d_sb = d_lo if g < 2 else d_hi
+                c0 = (g % 2) * 512
+                for kg in range(KG):
+                    nc.tensor.matmul_mx(
+                        out=h_ps[:],
+                        lhsT=a_sb[:, kg, 2 * m0 : 2 * (m0 + P)].bitcast(FP4X4),
+                        lhsT_scale=a_sc[:, kg, mt * P : (mt + 1) * P],
+                        rhs=d_sb[:, kg, 2 * c0 : 2 * (c0 + 512)].bitcast(FP4X4),
+                        rhs_scale=d_sc[:, kg, g * 512 : (g + 1) * 512],
+                        start=(kg == 0),
+                        stop=(kg == KG - 1),
+                    )
+
+        def op1(mt):
+            tmp = work.tile([P, FG, 512], F32, name="tmp")
+            tmps[mt] = tmp
+            for g in range(FG):
+                nc.vector.tensor_tensor(
+                    out=packed(tmp[:, g, :]),
+                    in0=upe(hs[mt, g][:]),
+                    in1=upe(nf_row[:, g * 512 : (g + 1) * 512]),
+                    op=ADD,
+                )
+
+        def op2_open(mt):
+            vs[mt] = work.tile([P, FG, 512], BF16, align_bytes=64, name="v_sb")
+
+        def op2(mt, g):
+            nc.vector.tensor_tensor(
+                out=packed(vs[mt][:, g, :]),
+                in0=packed(tmps[mt][:, g, :]),
+                in1=upe(slopes[mt][:, g * 512 : (g + 1) * 512]),
+                op=MULT,
+            )
+
+        def turn(mt, last=False):
+            words = vs[mt][:].rearrange("q g f -> q (g f)").bitcast(F32)
+            vq = work.tile([P, 1024], F32, align_bytes=64, name="vq")
+            vqs[mt] = vq
+            for b in range(2):
+                vt_ps = psum.tile([P, 4, P], F32, tag="vt", name="vt_ps")
+                for s in range(4):
+                    w0 = (4 * b + s) * P
+                    nc.tensor.transpose(vt_ps[:, s, :], words[:, w0 : w0 + P], ident_f[:])
+                dst = vq[:, 512 * b : 512 * (b + 1)].rearrange("p (g m u) -> p g m u", g=2, u=2)
+                src = vt_ps[:].rearrange("p (g u) m -> p g m u", u=2)
+                if last and b == 1:
+                    nc.vector.tensor_copy(out=dst, in_=src)
+                else:
+                    nc.scalar.copy(out=dst, in_=src)
+
+        def quant(mt):
+            code = work.tile([P, 512], U32, align_bytes=64, name="code")
+            csc = work.tile([P, 512], U8, align_bytes=64, name="csc")
+            codes[mt] = (code, csc)
+            nc.vector.quantize_mx(
+                out=code[:].bitcast(FP8X4), scales=csc[:], in_=vqs[mt][:].bitcast(BF16)
+            )
+
+        def s2(mt, nh, last=False):
+            code, csc = codes[mt]
+            y_ps = psum.tile([P, 512], F32, tag="y", name="y_ps")
+            for g in range(FG):
+                nc.tensor.matmul_mx(
+                    out=y_ps[:],
+                    lhsT=code[:, g * P : (g + 1) * P].bitcast(FP8X4),
+                    lhsT_scale=csc[:, g * P : (g + 1) * P],
+                    rhs=j_sb[:, g, 2048 * nh : 2048 * (nh + 1)].bitcast(FP8X4),
+                    rhs_scale=j_sc[4 * g : P, 512 * nh : 512 * (nh + 1)],
+                    start=(g == 0),
+                    stop=(g == FG - 1),
+                )
+            y_sb = ypool.tile([P, 512], F32, name="y_sb")
+            if last and nh == 1:
+                nc.vector.tensor_copy(out=y_sb[:], in_=y_ps[:])
+            else:
+                nc.scalar.copy(out=y_sb[:], in_=y_ps[:])
+            nc.sync.dma_start(
+                out=out[mt * P : (mt + 1) * P, 512 * nh : 512 * (nh + 1)], in_=y_sb[:]
+            )
+
+        s1(0)
+        op1(0)
+        op2_open(0)
+        for g in range(FG):
+            op2(0, g)
+        for i in range(MT - 1):
+            s1(i + 1)
+            op1(i + 1)
+            if i == 1:
+                s2(0, 0)
+                s2(0, 1)
+            turn(i)
+            op2_open(i + 1)
+            if i == 0:
+                quant(i)
+            for g in range(FG):
+                op2(i + 1, g)
+                if g == 1 and i > 0:
+                    quant(i)
+            if i > 1:
+                s2(i - 1, 0)
+                s2(i - 1, 1)
+        s2(MT - 2, 0)
+        turn(MT - 1, last=True)
+        quant(MT - 1)
+        s2(MT - 2, 1)
+        s2(MT - 1, 0, last=True)
+        s2(MT - 1, 1, last=True)

@@ -1,7 +1,6 @@
 from contextlib import ExitStack
 
 import concourse.mybir as mybir
-from concourse.masks import make_identity
 
 M, K, F, N = 1024, 1024, 2048, 1024
 FLOPS = 2 * M * K * F + 2 * M * F * N
@@ -15,6 +14,7 @@ FP4X4 = mybir.dt.float4_e2m1fn_x4
 FP8X4 = mybir.dt.float8_e4m3fn_x4
 ADD = mybir.AluOpType.add
 MULT = mybir.AluOpType.mult
+EQ = mybir.AluOpType.is_equal
 
 P = 128
 KG = K // 512
@@ -47,6 +47,7 @@ def tile_rounding_variance_propagation_s4_kernel(
         ident_h = keep.tile([P, P], BF16, align_bytes=64)
         ident_f = keep.tile([P, P], F32, align_bytes=64)
         slopes = [keep.tile([P, F], BF16, align_bytes=64, name="slope%d" % mt) for mt in range(MT)]
+        diff = keep.tile([P, P], F32, align_bytes=64)
         warm = keep.tile([P, 8], F32, align_bytes=64)
 
         nc.vector.memset(warm[:], 0.0)
@@ -59,24 +60,27 @@ def tile_rounding_variance_propagation_s4_kernel(
         asw = a_scales.bitcast(I32).rearrange("g r n -> r g n")
         dsw = d_scales.bitcast(I32).rearrange("g r n -> r g n")
         jsw = j_scales.bitcast(I32)
-        nc.sync.dma_start(out=nf_col[:], in_=noise_floor.rearrange("(p c) -> p c", c=16))
-        nc.sync.dma_start(out=a_lo[:].bitcast(I32), in_=aw[:, :, 0:256])
-        nc.sync.dma_start(out=d_lo[:].bitcast(I32), in_=dw[:, :, 0:512])
-        nc.sync.dma_start(out=d_hi[:].bitcast(I32), in_=dw[:, :, 512:1024])
-        make_identity(nc, ident_h[:])
+        nc.gpsimd.dma_start(out=a_lo[:].bitcast(I32), in_=aw[:, :, 0:256])
+        nc.gpsimd.dma_start(out=d_lo[:].bitcast(I32), in_=dw[:, :, 0:512])
+        nc.gpsimd.iota(
+            diff[:],
+            pattern=[[1, P]],
+            base=0,
+            channel_multiplier=-1,
+            allow_small_or_imprecise_dtypes=True,
+        )
+        nc.vector.tensor_scalar(ident_h[:], diff[:], 0.0, None, EQ)
+        nc.vector.tensor_scalar(ident_f[:], diff[:], 0.0, None, EQ)
+        nc.scalar.dma_start(out=nf_col[:], in_=noise_floor.rearrange("(p c) -> p c", c=16))
         for q in range(4):
             nc.scalar.dma_start(
                 out=d_sc[32 * q : 32 * q + 4, :, :].bitcast(I32), in_=dsw[4 * q : 4 * q + 4, :, :]
             )
         for q in range(4):
-            nc.gpsimd.dma_start(
+            nc.sync.dma_start(
                 out=a_sc[32 * q : 32 * q + 4, :, :].bitcast(I32), in_=asw[4 * q : 4 * q + 4, :, :]
             )
-        make_identity(nc, ident_f[:])
-        for q in range(4):
-            nc.gpsimd.dma_start(
-                out=j_sc[32 * q : 32 * q + 16, :].bitcast(I32), in_=jsw[:, 4 * q : 4 * q + 4, :]
-            )
+        nc.sync.dma_start(out=d_hi[:].bitcast(I32), in_=dw[:, :, 512:1024])
         nc.scalar.copy(out=warm[:, 4:5], in_=warm[:, 0:1])
 
         def load_slope(mt):
@@ -106,6 +110,11 @@ def tile_rounding_variance_propagation_s4_kernel(
                 nc.vector.tensor_copy(out=dst, in_=src)
             else:
                 nc.scalar.copy(out=dst, in_=src)
+
+        for q in range(4):
+            nc.scalar.dma_start(
+                out=j_sc[32 * q : 32 * q + 16, :].bitcast(I32), in_=jsw[:, 4 * q : 4 * q + 4, :]
+            )
 
         hs = {}
         tmps = {}
@@ -154,7 +163,8 @@ def tile_rounding_variance_propagation_s4_kernel(
             vs[mt] = work.tile([P, FG, 512], BF16, align_bytes=64, name="v_sb")
 
         def op2(mt, g):
-            nc.vector.tensor_tensor(
+            eng = nc.gpsimd if g == 0 else nc.vector
+            eng.tensor_tensor(
                 out=packed(vs[mt][:, g, :]),
                 in0=packed(tmps[mt][:, g, :]),
                 in1=upe(slopes[mt][:, g * 512 : (g + 1) * 512]),
@@ -177,34 +187,39 @@ def tile_rounding_variance_propagation_s4_kernel(
                 else:
                     nc.scalar.copy(out=dst, in_=src)
 
-        def quant(mt):
+        def quant(mt, parts=1):
             code = work.tile([P, 512], U32, align_bytes=64, name="code")
             csc = work.tile([P, 512], U8, align_bytes=64, name="csc")
             codes[mt] = (code, csc)
-            nc.vector.quantize_mx(
-                out=code[:].bitcast(FP8X4), scales=csc[:], in_=vqs[mt][:].bitcast(BF16)
-            )
+            width = 512 // parts
+            for k in range(parts):
+                w = slice(k * width, (k + 1) * width)
+                nc.vector.quantize_mx(
+                    out=code[:, w].bitcast(FP8X4),
+                    scales=csc[:, w],
+                    in_=vqs[mt][:, 2 * k * width : 2 * (k + 1) * width].bitcast(BF16),
+                )
 
-        def s2(mt, nh, last=False):
+        def s2(mt, n0, width=512, on_vector=False):
             code, csc = codes[mt]
-            y_ps = psum.tile([P, 512], F32, tag="y", name="y_ps")
+            y_ps = psum.tile([P, width], F32, tag="y", name="y_ps")
             for g in range(FG):
                 nc.tensor.matmul_mx(
                     out=y_ps[:],
                     lhsT=code[:, g * P : (g + 1) * P].bitcast(FP8X4),
                     lhsT_scale=csc[:, g * P : (g + 1) * P],
-                    rhs=j_sb[:, g, 2048 * nh : 2048 * (nh + 1)].bitcast(FP8X4),
-                    rhs_scale=j_sc[4 * g : P, 512 * nh : 512 * (nh + 1)],
+                    rhs=j_sb[:, g, 4 * n0 : 4 * (n0 + width)].bitcast(FP8X4),
+                    rhs_scale=j_sc[4 * g : P, n0 : n0 + width],
                     start=(g == 0),
                     stop=(g == FG - 1),
                 )
-            y_sb = ypool.tile([P, 512], F32, name="y_sb")
-            if last and nh == 1:
+            y_sb = ypool.tile([P, width], F32, name="y_sb")
+            if on_vector:
                 nc.vector.tensor_copy(out=y_sb[:], in_=y_ps[:])
             else:
                 nc.scalar.copy(out=y_sb[:], in_=y_ps[:])
             nc.sync.dma_start(
-                out=out[mt * P : (mt + 1) * P, 512 * nh : 512 * (nh + 1)], in_=y_sb[:]
+                out=out[mt * P : (mt + 1) * P, n0 : n0 + width], in_=y_sb[:]
             )
 
         s1(0)
@@ -217,21 +232,22 @@ def tile_rounding_variance_propagation_s4_kernel(
             op1(i + 1)
             if i == 1:
                 s2(0, 0)
-                s2(0, 1)
+                s2(0, 512)
             turn(i)
             op2_open(i + 1)
             if i == 0:
                 quant(i)
             for g in range(FG):
                 op2(i + 1, g)
-                if g == 1 and i > 0:
+                if g == 2 and i > 0:
                     quant(i)
             if i > 1:
                 s2(i - 1, 0)
-                s2(i - 1, 1)
+                s2(i - 1, 512)
         s2(MT - 2, 0)
         turn(MT - 1, last=True)
-        quant(MT - 1)
-        s2(MT - 2, 1)
-        s2(MT - 1, 0, last=True)
-        s2(MT - 1, 1, last=True)
+        quant(MT - 1, parts=2)
+        s2(MT - 2, 512)
+        s2(MT - 1, 0)
+        s2(MT - 1, 512, width=256)
+        s2(MT - 1, 768, width=256, on_vector=True)

@@ -36,11 +36,18 @@ def tile_rounding_variance_propagation_s4_kernel(
 
         a_lo = keep.tile([P, KG, 1024], U8, align_bytes=64)
         a_hi = keep.tile([P, KG, 1024], U8, align_bytes=64)
-        d_lo = keep.tile([P, KG, 2048], U8, align_bytes=64)
-        d_hi = keep.tile([P, KG, 2048], U8, align_bytes=64)
-        a_sc = keep.tile([P, KG, M], U8, align_bytes=64)
-        d_sc = keep.tile([P, KG, F], U8, align_bytes=64)
-        j_sb = keep.tile([P, FG, 4 * N], U8, align_bytes=64)
+        d_sb = [
+            keep.tile([P, KG, 1024], U8, align_bytes=64, name="d0"),
+            keep.tile([P, KG, 1024], U8, align_bytes=64, name="d1"),
+            keep.tile([P, KG, 2048], U8, align_bytes=64, name="d23"),
+        ]
+        as_lo = keep.tile([P, KG, 512], U8, align_bytes=64)
+        as_hi = keep.tile([P, KG, 512], U8, align_bytes=64)
+        ds_lo = keep.tile([P, KG, 1024], U8, align_bytes=64)
+        ds_hi = keep.tile([P, KG, 1024], U8, align_bytes=64)
+        j_sb = [
+            keep.tile([P, FG, 2048], U8, align_bytes=64, name="j%d" % nh) for nh in range(NH)
+        ]
         j_sc = keep.tile([P, N], U8, align_bytes=64)
         nf_col = keep.tile([P, 16], BF16, align_bytes=64)
         nf_row = keep.tile([P, F], BF16, align_bytes=64)
@@ -50,18 +57,37 @@ def tile_rounding_variance_propagation_s4_kernel(
         diff = keep.tile([P, P], F32, align_bytes=64)
         warm = keep.tile([P, 8], F32, align_bytes=64)
 
-        nc.vector.memset(warm[:], 0.0)
-        nc.vector.memset(d_sc[:].rearrange("p g n -> p (g n)").bitcast(I32), 0)
-        nc.vector.memset(a_sc[:].rearrange("p g n -> p (g n)").bitcast(I32), 0)
-        nc.vector.memset(j_sc[:].bitcast(I32), 0)
-
         aw = a_words.bitcast(I32).rearrange("g p n -> p g n")
         dw = d_words.bitcast(I32).rearrange("g p n -> p g n")
         asw = a_scales.bitcast(I32).rearrange("g r n -> r g n")
         dsw = d_scales.bitcast(I32).rearrange("g r n -> r g n")
+        jw = j_words.rearrange("g p n t -> g p (n t)").bitcast(I32).rearrange("g p n -> p g n")
         jsw = j_scales.bitcast(I32)
+
+        def zero(plane):
+            nc.vector.memset(plane[:].rearrange("p g n -> p (g n)").bitcast(I32), 0)
+
+        def load_rows(eng, plane, rows, q):
+            eng.dma_start(
+                out=plane[32 * q : 32 * q + 4, :, :].bitcast(I32), in_=rows[4 * q : 4 * q + 4, :, :]
+            )
+
+        def load_slope(mt):
+            nc.sync.dma_start(out=slopes[mt][:], in_=slope_sq[mt * P : (mt + 1) * P, :])
+
+        nc.gpsimd.dma_start(out=nf_col[:], in_=noise_floor.rearrange("(p c) -> p c", c=16))
         nc.gpsimd.dma_start(out=a_lo[:].bitcast(I32), in_=aw[:, :, 0:256])
-        nc.gpsimd.dma_start(out=d_lo[:].bitcast(I32), in_=dw[:, :, 0:512])
+        nc.sync.dma_start(out=d_sb[0][:].bitcast(I32), in_=dw[:, :, 0:256])
+        zero(ds_lo)
+        zero(as_lo)
+        zero(ds_hi)
+        zero(as_hi)
+        nc.vector.memset(warm[:], 0.0)
+        nc.vector.memset(j_sc[:].bitcast(I32), 0)
+        for q in range(4):
+            load_rows(nc.scalar, ds_lo, dsw[:, :, 0:256], q)
+        for q in range(4):
+            load_rows(nc.sync, as_lo, asw[:, :, 0:128], q)
         nc.gpsimd.iota(
             diff[:],
             pattern=[[1, P]],
@@ -71,30 +97,29 @@ def tile_rounding_variance_propagation_s4_kernel(
         )
         nc.vector.tensor_scalar(ident_h[:], diff[:], 0.0, None, EQ)
         nc.vector.tensor_scalar(ident_f[:], diff[:], 0.0, None, EQ)
-        nc.scalar.dma_start(out=nf_col[:], in_=noise_floor.rearrange("(p c) -> p c", c=16))
-        for q in range(4):
-            nc.scalar.dma_start(
-                out=d_sc[32 * q : 32 * q + 4, :, :].bitcast(I32), in_=dsw[4 * q : 4 * q + 4, :, :]
-            )
-        for q in range(4):
-            nc.sync.dma_start(
-                out=a_sc[32 * q : 32 * q + 4, :, :].bitcast(I32), in_=asw[4 * q : 4 * q + 4, :, :]
-            )
-        nc.sync.dma_start(out=d_hi[:].bitcast(I32), in_=dw[:, :, 512:1024])
         nc.scalar.copy(out=warm[:, 4:5], in_=warm[:, 0:1])
 
-        def load_slope(mt):
-            nc.sync.dma_start(out=slopes[mt][:], in_=slope_sq[mt * P : (mt + 1) * P, :])
-
+        nc.sync.dma_start(out=d_sb[1][:].bitcast(I32), in_=dw[:, :, 256:512])
+        for q in range(4):
+            load_rows(nc.sync, ds_hi, dsw[:, :, 256:512], q)
+        nc.sync.dma_start(out=d_sb[2][:].bitcast(I32), in_=dw[:, :, 512:1024])
         load_slope(0)
         load_slope(1)
-        nc.sync.dma_start(out=a_hi[:].bitcast(I32), in_=aw[:, :, 256:512])
-        for g in range(FG):
-            nc.sync.dma_start(
-                out=j_sb[:, g, :].bitcast(I32),
-                in_=j_words[g].rearrange("p n t -> p (n t)").bitcast(I32),
+        for q in range(4):
+            nc.gpsimd.dma_start(
+                out=j_sc[32 * q : 32 * q + 16, :].bitcast(I32), in_=jsw[:, 4 * q : 4 * q + 4, :]
             )
-        for mt in range(2, MT):
+        for nh in range(NH):
+            for b in range(2):
+                nc.sync.dma_start(
+                    out=j_sb[nh][:, 2 * b : 2 * b + 2, :].bitcast(I32),
+                    in_=jw[:, 2 * b : 2 * b + 2, 512 * nh : 512 * (nh + 1)],
+                )
+        load_slope(2)
+        nc.sync.dma_start(out=a_hi[:].bitcast(I32), in_=aw[:, :, 256:512])
+        for q in range(4):
+            load_rows(nc.gpsimd, as_hi, asw[:, :, 128:256], q)
+        for mt in range(3, MT):
             load_slope(mt)
 
         for h in range(2):
@@ -111,11 +136,6 @@ def tile_rounding_variance_propagation_s4_kernel(
             else:
                 nc.scalar.copy(out=dst, in_=src)
 
-        for q in range(4):
-            nc.scalar.dma_start(
-                out=j_sc[32 * q : 32 * q + 16, :].bitcast(I32), in_=jsw[:, 4 * q : 4 * q + 4, :]
-            )
-
         hs = {}
         tmps = {}
         vs = {}
@@ -130,20 +150,21 @@ def tile_rounding_variance_propagation_s4_kernel(
             return ap.rearrange("q (u p e) -> q u p e", u=2, e=2)
 
         def s1(mt):
-            a_sb = a_lo if mt < 4 else a_hi
+            a_sb, as_sb = (a_lo, as_lo) if mt < 4 else (a_hi, as_hi)
             m0 = (mt % 4) * P
             for g in range(FG):
                 h_ps = psum.tile([P, 512], F32, tag="h", bufs=4, name="h_ps")
                 hs[mt, g] = h_ps
-                d_sb = d_lo if g < 2 else d_hi
-                c0 = (g % 2) * 512
+                d_g, ds_g = d_sb[min(g, 2)], ds_lo if g < 2 else ds_hi
+                c0 = 512 if g == 3 else 0
+                s0 = (g % 2) * 512
                 for kg in range(KG):
                     nc.tensor.matmul_mx(
                         out=h_ps[:],
                         lhsT=a_sb[:, kg, 2 * m0 : 2 * (m0 + P)].bitcast(FP4X4),
-                        lhsT_scale=a_sc[:, kg, mt * P : (mt + 1) * P],
-                        rhs=d_sb[:, kg, 2 * c0 : 2 * (c0 + 512)].bitcast(FP4X4),
-                        rhs_scale=d_sc[:, kg, g * 512 : (g + 1) * 512],
+                        lhsT_scale=as_sb[:, kg, m0 : m0 + P],
+                        rhs=d_g[:, kg, 2 * c0 : 2 * (c0 + 512)].bitcast(FP4X4),
+                        rhs_scale=ds_g[:, kg, s0 : s0 + 512],
                         start=(kg == 0),
                         stop=(kg == KG - 1),
                     )
@@ -163,8 +184,7 @@ def tile_rounding_variance_propagation_s4_kernel(
             vs[mt] = work.tile([P, FG, 512], BF16, align_bytes=64, name="v_sb")
 
         def op2(mt, g):
-            eng = nc.gpsimd if g == 0 else nc.vector
-            eng.tensor_tensor(
+            nc.vector.tensor_tensor(
                 out=packed(vs[mt][:, g, :]),
                 in0=packed(tmps[mt][:, g, :]),
                 in1=upe(slopes[mt][:, g * 512 : (g + 1) * 512]),
@@ -208,7 +228,7 @@ def tile_rounding_variance_propagation_s4_kernel(
                     out=y_ps[:],
                     lhsT=code[:, g * P : (g + 1) * P].bitcast(FP8X4),
                     lhsT_scale=csc[:, g * P : (g + 1) * P],
-                    rhs=j_sb[:, g, 4 * n0 : 4 * (n0 + width)].bitcast(FP8X4),
+                    rhs=j_sb[n0 // 512][:, g, 4 * (n0 % 512) : 4 * (n0 % 512 + width)].bitcast(FP8X4),
                     rhs_scale=j_sc[4 * g : P, n0 : n0 + width],
                     start=(g == 0),
                     stop=(g == FG - 1),
@@ -239,7 +259,7 @@ def tile_rounding_variance_propagation_s4_kernel(
                 quant(i)
             for g in range(FG):
                 op2(i + 1, g)
-                if g == 2 and i > 0:
+                if g == 1 and i > 0:
                     quant(i)
             if i > 1:
                 s2(i - 1, 0)

@@ -75,8 +75,8 @@ def tile_rounding_variance_propagation_s4_kernel(
         def load_slope(mt):
             nc.sync.dma_start(out=slopes[mt][:], in_=slope_sq[mt * P : (mt + 1) * P, :])
 
-        nc.gpsimd.dma_start(out=nf_col[:], in_=noise_floor.rearrange("(p c) -> p c", c=16))
-        nc.gpsimd.dma_start(out=a_lo[:].bitcast(I32), in_=aw[:, :, 0:256])
+        nc.scalar.dma_start(out=nf_col[:], in_=noise_floor.rearrange("(p c) -> p c", c=16))
+        nc.sync.dma_start(out=a_lo[:].bitcast(I32), in_=aw[:, :, 0:256])
         nc.sync.dma_start(out=d_sb[0][:].bitcast(I32), in_=dw[:, :, 0:256])
         zero(ds_lo)
         zero(as_lo)
@@ -106,7 +106,7 @@ def tile_rounding_variance_propagation_s4_kernel(
         load_slope(0)
         load_slope(1)
         for q in range(4):
-            nc.gpsimd.dma_start(
+            nc.sync.dma_start(
                 out=j_sc[32 * q : 32 * q + 16, :].bitcast(I32), in_=jsw[:, 4 * q : 4 * q + 4, :]
             )
         for nh in range(NH):
@@ -118,7 +118,7 @@ def tile_rounding_variance_propagation_s4_kernel(
         load_slope(2)
         nc.sync.dma_start(out=a_hi[:].bitcast(I32), in_=aw[:, :, 256:512])
         for q in range(4):
-            load_rows(nc.gpsimd, as_hi, asw[:, :, 128:256], q)
+            load_rows(nc.sync, as_hi, asw[:, :, 128:256], q)
         for mt in range(3, MT):
             load_slope(mt)
 
@@ -184,7 +184,8 @@ def tile_rounding_variance_propagation_s4_kernel(
             vs[mt] = work.tile([P, FG, 512], BF16, align_bytes=64, name="v_sb")
 
         def op2(mt, g):
-            nc.vector.tensor_tensor(
+            eng = nc.gpsimd if g == 0 else nc.vector
+            eng.tensor_tensor(
                 out=packed(vs[mt][:, g, :]),
                 in0=packed(tmps[mt][:, g, :]),
                 in1=upe(slopes[mt][:, g * 512 : (g + 1) * 512]),
@@ -220,9 +221,9 @@ def tile_rounding_variance_propagation_s4_kernel(
                     in_=vqs[mt][:, 2 * k * width : 2 * (k + 1) * width].bitcast(BF16),
                 )
 
-        def s2(mt, n0, width=512, on_vector=False):
+        def s2(mt, n0, width=512, on_vector=False, bank=("y", 2)):
             code, csc = codes[mt]
-            y_ps = psum.tile([P, width], F32, tag="y", name="y_ps")
+            y_ps = psum.tile([P, width], F32, tag=bank[0], bufs=bank[1], name="y_ps")
             for g in range(FG):
                 nc.tensor.matmul_mx(
                     out=y_ps[:],
@@ -259,15 +260,15 @@ def tile_rounding_variance_propagation_s4_kernel(
                 quant(i)
             for g in range(FG):
                 op2(i + 1, g)
-                if g == 1 and i > 0:
+                if g == 3 and i > 0:
                     quant(i)
             if i > 1:
                 s2(i - 1, 0)
                 s2(i - 1, 512)
-        s2(MT - 2, 0)
         turn(MT - 1, last=True)
         quant(MT - 1, parts=2)
-        s2(MT - 2, 512)
-        s2(MT - 1, 0)
-        s2(MT - 1, 512, width=256)
-        s2(MT - 1, 768, width=256, on_vector=True)
+        s2(MT - 2, 0)
+        s2(MT - 2, 512, on_vector=True)
+        s2(MT - 1, 0, bank=("h", 4))
+        s2(MT - 1, 512, width=256, on_vector=True, bank=("h", 4))
+        s2(MT - 1, 768, width=256, bank=("h", 4))

from contextlib import ExitStack

import concourse.mybir as mybir

M, K, F, N = 1024, 1024, 2048, 1024
FLOPS = 2 * M * K * F + 2 * M * F * N

F32 = mybir.dt.float32
BF16 = mybir.dt.bfloat16
I32 = mybir.dt.int32
U32 = mybir.dt.uint32
U8 = mybir.dt.uint8
FP4X4 = mybir.dt.float4_e2m1fn_x4
FP8X4 = mybir.dt.float8_e4m3fn_x4
ADD = mybir.AluOpType.add
MULT = mybir.AluOpType.mult
EQ = mybir.AluOpType.is_equal

P = 128
KG = K // 512
FG = F // 512
MT = M // P
NH = N // 512


def tile_rounding_variance_propagation_s4_kernel(
    tc, a_words, a_scales, d_words, d_scales, noise_floor, slope_sq, j_words, j_scales, out
):
    nc = tc.nc
    with ExitStack() as ctx:
        keep = ctx.enter_context(tc.tile_pool(name="keep", bufs=1))
        work = ctx.enter_context(tc.tile_pool(name="work", bufs=2))
        ypool = ctx.enter_context(tc.tile_pool(name="ypool", bufs=4))
        psum = ctx.enter_context(tc.psum_pool(name="psum", bufs=2))
        ctx.enter_context(tc.manual_schedule())

        a_lo = keep.tile([P, KG, 1024], U8, align_bytes=64)
        a_hi = keep.tile([P, KG, 1024], U8, align_bytes=64)
        d_sb = [
            keep.tile([P, KG, 1024], U8, align_bytes=64, name="d0"),
            keep.tile([P, KG, 1024], U8, align_bytes=64, name="d1"),
            keep.tile([P, KG, 2048], U8, align_bytes=64, name="d23"),
        ]
        as_lo = keep.tile([P, KG, 512], U8, align_bytes=64)
        as_hi = keep.tile([P, KG, 512], U8, align_bytes=64)
        ds_lo = keep.tile([P, KG, 1024], U8, align_bytes=64)
        ds_hi = keep.tile([P, KG, 1024], U8, align_bytes=64)
        j_sb = [
            keep.tile([P, FG, 2048], U8, align_bytes=64, name="j%d" % nh) for nh in range(NH)
        ]
        j_sc = keep.tile([P, N], U8, align_bytes=64)
        nf_col = keep.tile([P, 16], BF16, align_bytes=64)
        nf_row = keep.tile([P, F], BF16, align_bytes=64)
        ident_h = keep.tile([P, P], BF16, align_bytes=64)
        ident_f = keep.tile([P, P], F32, align_bytes=64)
        slopes = [keep.tile([P, F], BF16, align_bytes=64, name="slope%d" % mt) for mt in range(MT)]
        diff = keep.tile([P, P], F32, align_bytes=64)
        warm = keep.tile([P, 8], F32, align_bytes=64)

        aw = a_words.bitcast(I32).rearrange("g p n -> p g n")
        dw = d_words.bitcast(I32).rearrange("g p n -> p g n")
        asw = a_scales.bitcast(I32).rearrange("g r n -> r g n")
        dsw = d_scales.bitcast(I32).rearrange("g r n -> r g n")
        jw = j_words.rearrange("g p n t -> g p (n t)").bitcast(I32).rearrange("g p n -> p g n")
        jsw = j_scales.bitcast(I32)

        def zero(plane):
            nc.vector.memset(plane[:].rearrange("p g n -> p (g n)").bitcast(I32), 0)

        def load_rows(eng, plane, rows, q):
            eng.dma_start(
                out=plane[32 * q : 32 * q + 4, :, :].bitcast(I32), in_=rows[4 * q : 4 * q + 4, :, :]
            )

        def load_slope(mt):
            nc.sync.dma_start(out=slopes[mt][:], in_=slope_sq[mt * P : (mt + 1) * P, :])

        nc.scalar.dma_start(out=nf_col[:], in_=noise_floor.rearrange("(p c) -> p c", c=16))
        nc.sync.dma_start(out=a_lo[:].bitcast(I32), in_=aw[:, :, 0:256])
        nc.sync.dma_start(out=d_sb[0][:].bitcast(I32), in_=dw[:, :, 0:256])
        zero(ds_lo)
        zero(as_lo)
        zero(ds_hi)
        zero(as_hi)
        nc.vector.memset(warm[:], 0.0)
        nc.vector.memset(j_sc[:].bitcast(I32), 0)
        for q in range(4):
            load_rows(nc.scalar, ds_lo, dsw[:, :, 0:256], q)
        for q in range(4):
            load_rows(nc.sync, as_lo, asw[:, :, 0:128], q)
        nc.gpsimd.iota(
            diff[:],
            pattern=[[1, P]],
            base=0,
            channel_multiplier=-1,
            allow_small_or_imprecise_dtypes=True,
        )
        nc.vector.tensor_scalar(ident_h[:], diff[:], 0.0, None, EQ)
        nc.vector.tensor_scalar(ident_f[:], diff[:], 0.0, None, EQ)
        nc.scalar.copy(out=warm[:, 4:5], in_=warm[:, 0:1])

        nc.sync.dma_start(out=d_sb[1][:].bitcast(I32), in_=dw[:, :, 256:512])
        for q in range(4):
            load_rows(nc.sync, ds_hi, dsw[:, :, 256:512], q)
        nc.sync.dma_start(out=d_sb[2][:].bitcast(I32), in_=dw[:, :, 512:1024])
        load_slope(0)
        load_slope(1)
        for q in range(4):
            nc.sync.dma_start(
                out=j_sc[32 * q : 32 * q + 16, :].bitcast(I32), in_=jsw[:, 4 * q : 4 * q + 4, :]
            )
        for nh in range(NH):
            for b in range(2):
                nc.sync.dma_start(
                    out=j_sb[nh][:, 2 * b : 2 * b + 2, :].bitcast(I32),
                    in_=jw[:, 2 * b : 2 * b + 2, 512 * nh : 512 * (nh + 1)],
                )
        load_slope(2)
        nc.sync.dma_start(out=a_hi[:].bitcast(I32), in_=aw[:, :, 256:512])
        for q in range(4):
            load_rows(nc.sync, as_hi, asw[:, :, 128:256], q)
        for mt in range(3, MT):
            load_slope(mt)

        for h in range(2):
            nf_ps = psum.tile([P, 8, P], BF16, tag="vt", name="nf_ps")
            for c in range(8):
                col = 8 * h + c
                nc.tensor.transpose(
                    nf_ps[:, c, :], nf_col[:, col : col + 1].to_broadcast([P, P]), ident_h[:]
                )
            dst = nf_row[:].rearrange("q (p c) -> q p c", c=16)[:, :, 8 * h : 8 * h + 8]
            src = nf_ps[:].rearrange("q c p -> q p c")
            if h == 0:
                nc.vector.tensor_copy(out=dst, in_=src)
            else:
                nc.scalar.copy(out=dst, in_=src)

        hs = {}
        tmps = {}
        vs = {}
        vts = {}
        vqs = {}
        codes = {}

        def upe(ap):
            return ap.rearrange("q (p u e) -> q u p e", u=2, e=2)

        def packed(ap):
            return ap.rearrange("q (u p e) -> q u p e", u=2, e=2)

        def s1(mt):
            a_sb, as_sb = (a_lo, as_lo) if mt < 4 else (a_hi, as_hi)
            m0 = (mt % 4) * P
            for g in range(FG):
                h_ps = psum.tile([P, 512], F32, tag="h", bufs=4, name="h_ps")
                hs[mt, g] = h_ps
                d_g, ds_g = d_sb[min(g, 2)], ds_lo if g < 2 else ds_hi
                c0 = 512 if g == 3 else 0
                s0 = (g % 2) * 512
                for kg in range(KG):
                    nc.tensor.matmul_mx(
                        out=h_ps[:],
                        lhsT=a_sb[:, kg, 2 * m0 : 2 * (m0 + P)].bitcast(FP4X4),
                        lhsT_scale=as_sb[:, kg, m0 : m0 + P],
                        rhs=d_g[:, kg, 2 * c0 : 2 * (c0 + 512)].bitcast(FP4X4),
                        rhs_scale=ds_g[:, kg, s0 : s0 + 512],
                        start=(kg == 0),
                        stop=(kg == KG - 1),
                    )

        def op1(mt):
            tmp = work.tile([P, FG, 512], F32, name="tmp")
            tmps[mt] = tmp
            for g in range(FG):
                nc.vector.tensor_tensor(
                    out=packed(tmp[:, g, :]),
                    in0=upe(hs[mt, g][:]),
                    in1=upe(nf_row[:, g * 512 : (g + 1) * 512]),
                    op=ADD,
                )

        def op2_open(mt):
            vs[mt] = work.tile([P, FG, 512], BF16, align_bytes=64, name="v_sb")

        def op2(mt, g):
            eng = nc.gpsimd if g == 0 else nc.vector
            eng.tensor_tensor(
                out=packed(vs[mt][:, g, :]),
                in0=packed(tmps[mt][:, g, :]),
                in1=upe(slopes[mt][:, g * 512 : (g + 1) * 512]),
                op=MULT,
            )

        def turn(mt, last=False):
            words = vs[mt][:].rearrange("q g f -> q (g f)").bitcast(F32)
            vq = work.tile([P, 1024], F32, align_bytes=64, name="vq")
            vqs[mt] = vq
            for b in range(2):
                vt_ps = psum.tile([P, 4, P], F32, tag="vt", name="vt_ps")
                for s in range(4):
                    w0 = (4 * b + s) * P
                    nc.tensor.transpose(vt_ps[:, s, :], words[:, w0 : w0 + P], ident_f[:])
                dst = vq[:, 512 * b : 512 * (b + 1)].rearrange("p (g m u) -> p g m u", g=2, u=2)
                src = vt_ps[:].rearrange("p (g u) m -> p g m u", u=2)
                if last and b == 1:
                    nc.vector.tensor_copy(out=dst, in_=src)
                else:
                    nc.scalar.copy(out=dst, in_=src)

        def quant(mt, parts=1):
            code = work.tile([P, 512], U32, align_bytes=64, name="code")
            csc = work.tile([P, 512], U8, align_bytes=64, name="csc")
            codes[mt] = (code, csc)
            width = 512 // parts
            for k in range(parts):
                w = slice(k * width, (k + 1) * width)
                nc.vector.quantize_mx(
                    out=code[:, w].bitcast(FP8X4),
                    scales=csc[:, w],
                    in_=vqs[mt][:, 2 * k * width : 2 * (k + 1) * width].bitcast(BF16),
                )

        def s2(mt, n0, width=512, on_vector=False, bank=("y", 2)):
            code, csc = codes[mt]
            y_ps = psum.tile([P, width], F32, tag=bank[0], bufs=bank[1], name="y_ps")
            for g in range(FG):
                nc.tensor.matmul_mx(
                    out=y_ps[:],
                    lhsT=code[:, g * P : (g + 1) * P].bitcast(FP8X4),
                    lhsT_scale=csc[:, g * P : (g + 1) * P],
                    rhs=j_sb[n0 // 512][:, g, 4 * (n0 % 512) : 4 * (n0 % 512 + width)].bitcast(FP8X4),
                    rhs_scale=j_sc[4 * g : P, n0 : n0 + width],
                    start=(g == 0),
                    stop=(g == FG - 1),
                )
            y_sb = ypool.tile([P, width], F32, name="y_sb")
            if on_vector:
                nc.vector.tensor_copy(out=y_sb[:], in_=y_ps[:])
            else:
                nc.scalar.copy(out=y_sb[:], in_=y_ps[:])
            nc.sync.dma_start(
                out=out[mt * P : (mt + 1) * P, n0 : n0 + width], in_=y_sb[:]
            )

        s1(0)
        op1(0)
        op2_open(0)
        for g in range(FG):
            op2(0, g)
        for i in range(MT - 1):
            s1(i + 1)
            op1(i + 1)
            if i == 1:
                s2(0, 0)
                s2(0, 512)
            turn(i)
            op2_open(i + 1)
            if i == 0:
                quant(i)
            for g in range(FG):
                op2(i + 1, g)
                if g == 3 and i > 0:
                    quant(i)
            if i > 1:
                s2(i - 1, 0)
                s2(i - 1, 512)
        turn(MT - 1, last=True)
        quant(MT - 1, parts=2)
        s2(MT - 2, 0)
        s2(MT - 2, 512, on_vector=True)
        s2(MT - 1, 0, bank=("h", 4))
        s2(MT - 1, 512, width=256, on_vector=True, bank=("h", 4))
        s2(MT - 1, 768, width=256, bank=("h", 4))
